import numpy as np
import ml_dtypes


def mxq(x, axis, fmt="e4m3"):
    dtype, down = {"e4m3": (ml_dtypes.float8_e4m3fn, 7), "e5m2": (ml_dtypes.float8_e5m2, 14)}[fmt]
    v = np.moveaxis(np.asarray(x, np.float32).astype(ml_dtypes.bfloat16).astype(np.float64), axis, -1)
    blocks = v.reshape(v.shape[:-1] + (-1, 32))
    amax = np.abs(blocks).max(-1, keepdims=True)
    byte = np.maximum(np.where(amax > 0, np.frexp(amax)[1] - 1 + 127, 0) - down, 1)
    scale = np.exp2(byte - 127.0)
    codes = (blocks / scale).astype(np.float32).astype(dtype).astype(np.float64)
    return np.moveaxis((codes * scale).reshape(v.shape), -1, axis)


WIDE = False


def mx_kscale(k):
    if not WIDE:
        return np.ones(k)
    levels = np.array([10, -10, 5, -5, 0])
    if k % 512:
        return np.exp2(np.random.permutation(np.resize(levels, k // 32))).repeat(32)
    a = np.empty((k // 512, 16))
    for p in range(k // 512):
        a[p, :8] = np.random.permutation(np.resize(levels, 8))
        for g in range(8):
            far = levels[np.abs(levels - a[p, g]) >= 10]
            a[p, g + 8] = far[np.random.randint(len(far))]
    return np.exp2(a.ravel()).repeat(32)


def f64(x):
    return np.asarray(x).astype(np.float64)


def striped(idx):
    return np.tile(idx.reshape(-1, 16).T, (8, 1)).astype(np.uint16)


def unstriped(offs):
    return offs[:16].T.reshape(-1).astype(np.int64)


def pack_weight(w):
    k, n = w.shape
    w = f64(np.asarray(w, np.float32).astype(ml_dtypes.bfloat16)).reshape(k // 32, 32, n)
    amax = np.abs(w).max(1)
    byte = np.clip(np.where(amax > 0, np.frexp(amax)[1] - 1 + 127 - 7, 1), 1, 254)
    scaled = (w * np.exp2(127.0 - byte)[:, None, :]).reshape(k, n).astype(np.float32)
    words = np.ascontiguousarray(scaled.reshape(k // 512, 128, 4, n).transpose(0, 1, 3, 2)).astype(ml_dtypes.float8_e4m3fn).view(np.uint8)
    return words, np.ascontiguousarray(byte.astype(np.uint8).reshape(k // 512, 16, n))


def unpack_weight(words, scales):
    g, p, n, _ = words.shape
    vals = np.ascontiguousarray(words).view(ml_dtypes.float8_e4m3fn).astype(np.float64) * np.repeat(np.exp2(scales.astype(np.float64) - 127.0), 8, axis=1)[..., None]
    return vals.transpose(0, 1, 3, 2).reshape(g * 512, n)


def planes(y):
    n, m = y.shape
    v = y.astype(np.float32).astype(ml_dtypes.bfloat16).astype(np.float64).reshape(n // 32, 32, m)
    top = np.abs(v).max(1)
    byte = np.clip(np.where(top > 0, np.frexp(top)[1] - 1 + 127 - 7, 1), 1, 254)
    codes = (v * np.exp2(127.0 - byte)[:, None, :]).reshape(n, m).astype(np.float32).astype(ml_dtypes.float8_e4m3fn).view(np.uint8)
    words = codes.reshape(n // 512, 128, 4, m).transpose(0, 1, 3, 2)
    return np.ascontiguousarray(words), np.ascontiguousarray(byte.astype(np.uint8).reshape(n // 512, 16, m))


def silu(v):
    return v / (1.0 + np.exp(-np.maximum(v, -700.0)))


K, T, S, H = 1024, 4096, 1024, 512


def setup_inputs():
    n = np.random.standard_normal
    s = mx_kscale(K)[:, None]
    u = mx_kscale(H)
    packed_xT = pack_weight(n((K, T)) * s)
    return {
        "x_words": packed_xT[0],
        "x_scales": packed_xT[1],
        "w1": (n((K, H)) / np.sqrt(K) / s * u).astype(np.float32),
        "w2": (n((H, H)) / np.sqrt(H) / u[:, None]).astype(np.float32),
        "turn": (np.random.uniform(0.5, 1.5, (H, 1)) * u[:, None]).astype(np.float32),
        "offs": striped(np.random.permutation(T)[:S]),
    }


def reference(x_words, x_scales, w1, w2, turn, offs):
    xq = unpack_weight(x_words, x_scales)[:, unstriped(offs)]
    h = mxq(f64(w1), 0, "e4m3").T @ xq
    g = silu(h)
    y = mxq(f64(w2), 0, "e4m3").T @ mxq(g, 0, "e4m3")
    out_0 = h + f64(turn) * y
    return (out_0,) + planes(out_0)

@@ -1,0 +1,224 @@
+from contextlib import ExitStack
+
+import concourse.mybir as mybir
+
+F32 = mybir.dt.float32
+BF16 = mybir.dt.bfloat16
+I32 = mybir.dt.int32
+U32 = mybir.dt.uint32
+U16 = mybir.dt.uint16
+U8 = mybir.dt.uint8
+FP8X4 = mybir.dt.float8_e4m3fn_x4
+SILU = mybir.ActivationFunctionType.Silu
+MULT = mybir.AluOpType.mult
+ADD = mybir.AluOpType.add
+
+P = 128
+PACK = 4
+K, T, S, H = 1024, 4096, 1024, 512
+PASSES = K // (P * PACK)
+CHUNK = 128
+GROUP = 256
+HALF = 512
+FLOPS = 2 * K * H * S + 2 * H * H * S
+
+
+def deal_weights(engine_copy, grouped, raw):
+    engine_copy(
+        out=grouped[:].rearrange("p (t m j) -> p m j t", t=PACK, j=PACK),
+        in_=raw[:].rearrange("p j (m t) -> p m j t", t=PACK),
+    )
+
+
+def tile_picked_zres_silu_po_kernel(
+    tc, x_words, x_scales, w1, w2, turn, offs, out_0, out_1, out_2
+):
+    nc = tc.nc
+    with ExitStack() as ctx:
+        keep = ctx.enter_context(tc.tile_pool(name="keep", bufs=1))
+        hps = ctx.enter_context(tc.psum_pool(name="hps", bufs=4))
+        yps = ctx.enter_context(tc.psum_pool(name="yps", bufs=4))
+
+        offsets = keep.tile([P, S // 16], U16, name="offsets")
+        w1_raw = [keep.tile([P, PACK, H], F32, name="w1_raw%d" % o) for o in range(PASSES)]
+        w2_raw = keep.tile([P, PACK, H], F32, name="w2_raw")
+        word_table = [keep.tile([P, T], I32, name="word_table%d" % o) for o in range(PASSES)]
+        scale_table = keep.tile([P, T], U8, name="scale_table")
+        turn_sb = keep.tile([P, PACK], F32, name="turn_sb")
+
+        warm = keep.tile([P, 8], F32, name="warm")
+        warm_out = keep.tile([P, 8], F32, name="warm_out")
+        nc.vector.memset(warm[:], 0.0)
+        nc.scalar.activation(warm_out[:], warm[:], SILU)
+
+        nc.vector.memset(scale_table[:].bitcast(I32), 0)
+
+        def load_words(o):
+            nc.sync.dma_start(out=word_table[o][:], in_=x_words[o].rearrange("p n t -> p (n t)").bitcast(I32))
+
+        load_words(0)
+        nc.sync.dma_start(offsets[:], offs)
+        for q in range(4):
+            nc.sync.dma_start(
+                out=scale_table[32 * q : 32 * q + 4 * PASSES, :].bitcast(I32),
+                in_=x_scales[:, 4 * q : 4 * q + 4, :].bitcast(I32),
+            )
+        for o in range(PASSES):
+            nc.sync.dma_start(out=w1_raw[o][:], in_=w1[512 * o : 512 * (o + 1), :].rearrange("(p j) c -> p j c", j=PACK))
+        load_words(1)
+        nc.sync.dma_start(out=w2_raw[:], in_=w2.rearrange("(p j) c -> p j c", j=PACK))
+        nc.sync.dma_start(out=turn_sb[:], in_=turn.rearrange("(p t) o -> p (t o)", t=PACK))
+
+        x_first = keep.tile([P, S], U32, name="x_first", align_bytes=64)
+        nc.vector.tensor_copy(x_first[:], word_table[0][:].bitcast(U32).indirect(offsets[:]))
+        x_sc = keep.tile([P, S], U8, name="x_sc", align_bytes=64)
+        nc.vector.tensor_copy(x_sc[:], scale_table[:].indirect(offsets[:]))
+
+        w1_bf = [keep.tile([P, H * PACK], BF16, name="w1_bf%d" % o, align_bytes=64) for o in range(PASSES)]
+        deal_weights(nc.scalar.copy, w1_bf[0], w1_raw[0])
+        deal_weights(nc.vector.tensor_copy, w1_bf[1], w1_raw[1])
+        w1_codes, w1_scales = [], []
+        for o in range(PASSES):
+            codes = keep.tile([P, H], U32, name="w1_codes%d" % o, align_bytes=64)
+            scales = keep.tile([P, H], U8, name="w1_scales%d" % o, align_bytes=64)
+            nc.vector.quantize_mx(out=codes[:].bitcast(FP8X4), scales=scales[:], in_=w1_bf[o][:])
+            w1_codes.append(codes)
+            w1_scales.append(scales)
+
+        x_second = []
+        for hf in range(S // HALF):
+            tile = keep.tile([P, HALF], U32, name="x_second%d" % hf, align_bytes=64)
+            cols = slice(hf * HALF // 16, (hf + 1) * HALF // 16)
+            nc.vector.tensor_copy(tile[:], word_table[1][:].bitcast(U32).indirect(offsets[:, cols]))
+            x_second.append(tile)
+
+        warm_bank = yps.tile([P, 2, GROUP], F32, name="y_bank")
+        for rep in range(3):
+            nc.tensor.matmul_mx(
+                out=warm_bank[:].rearrange("p u n -> p (u n)"),
+                lhsT=w1_codes[1][:, 0:P].bitcast(FP8X4),
+                lhsT_scale=w1_scales[1][:, 0:P],
+                rhs=x_first[:, 0:HALF].bitcast(FP8X4),
+                rhs_scale=x_sc[:, 0:HALF],
+                start=True,
+                stop=True,
+            )
+
+        out_rows = out_0.rearrange("(p t) n -> p t n", t=PACK)
+        out_words = out_1[0].rearrange("p n t -> p (n t)").bitcast(I32)
+        out_sc = keep.tile([P, S], U8, name="out_sc", align_bytes=64)
+
+        groups = S // GROUP
+        g_bf = [keep.tile([P, GROUP * PACK], BF16, name="g_bf%d" % g, align_bytes=64) for g in range(groups)]
+        g_codes = [keep.tile([P, GROUP], U32, name="g_codes%d" % g, align_bytes=64) for g in range(groups)]
+        g_scales = [keep.tile([P, GROUP], U8, name="g_scales%d" % g, align_bytes=64) for g in range(groups)]
+        h_sb = [keep.tile([P, PACK, GROUP], F32, name="h_sb%d" % g) for g in range(groups)]
+        res = [keep.tile([P, PACK, GROUP], F32, name="res%d" % g) for g in range(groups)]
+        res_bf = [keep.tile([P, GROUP * PACK], BF16, name="res_bf%d" % g, align_bytes=64) for g in range(groups)]
+        w2_bf = keep.tile([P, H * PACK], BF16, name="w2_bf", align_bytes=64)
+        w2_codes = keep.tile([P, H], U32, name="w2_codes", align_bytes=64)
+        w2_scales = keep.tile([P, H], U8, name="w2_scales", align_bytes=64)
+        h_banks = {}
+
+        def project(g):
+            for c in range(GROUP // CHUNK):
+                n0 = g * GROUP + c * CHUNK
+                bank = hps.tile([P, PACK, CHUNK], F32, name="h_bank")
+                h_banks[(g, c)] = bank
+                for t in range(PACK):
+                    m = slice(t * P, (t + 1) * P)
+                    for o in range(PASSES):
+                        if o == 0:
+                            words = x_first[:, n0 : n0 + CHUNK]
+                        else:
+                            words = x_second[n0 // HALF][:, n0 % HALF : n0 % HALF + CHUNK]
+                        nc.tensor.matmul_mx(
+                            out=bank[:, t, :],
+                            lhsT=w1_codes[o][:, m].bitcast(FP8X4),
+                            lhsT_scale=w1_scales[o][:, m],
+                            rhs=words.bitcast(FP8X4),
+                            rhs_scale=x_sc[4 * o : P, n0 : n0 + CHUNK],
+                            start=(o == 0),
+                            stop=(o == PASSES - 1),
+                        )
+                nc.scalar.activation(
+                    g_bf[g][:, c * CHUNK * PACK : (c + 1) * CHUNK * PACK].rearrange("p (n t) -> p n t", t=PACK),
+                    bank[:].rearrange("p t n -> p n t"),
+                    SILU,
+                )
+
+        def keep_h(g):
+            for c in range(GROUP // CHUNK):
+                nc.scalar.copy(out=h_sb[g][:, :, c * CHUNK : (c + 1) * CHUNK], in_=h_banks[(g, c)][:])
+
+        def quantise_g(g):
+            nc.vector.quantize_mx(out=g_codes[g][:].bitcast(FP8X4), scales=g_scales[g][:], in_=g_bf[g][:])
+
+        def branch(g):
+            cols = slice(g * GROUP, (g + 1) * GROUP)
+            for pair in range(PACK // 2):
+                bank = yps.tile([P, 2, GROUP], F32, name="y_bank")
+                for u in range(2):
+                    t = 2 * pair + u
+                    m = slice(t * P, (t + 1) * P)
+                    nc.tensor.matmul_mx(
+                        out=bank[:, u, :],
+                        lhsT=w2_codes[:, m].bitcast(FP8X4),
+                        lhsT_scale=w2_scales[:, m],
+                        rhs=g_codes[g][:].bitcast(FP8X4),
+                        rhs_scale=g_scales[g][:],
+                        start=True,
+                        stop=True,
+                    )
+                for u in range(2):
+                    t = 2 * pair + u
+                    nc.vector.scalar_tensor_tensor(
+                        out=res[g][:, t, :], in0=bank[:, u, :], scalar=turn_sb[:, t : t + 1], in1=h_sb[g][:, t, :], op0=MULT, op1=ADD
+                    )
+            nc.sync.dma_start(out=out_rows[:, :, cols], in_=res[g][:])
+
+        def round_result(copy, g, n0, n1):
+            copy(
+                out=res_bf[g][:, n0 * PACK : n1 * PACK].rearrange("p (c i t) -> p c t i", i=4, t=PACK),
+                in_=res[g][:, :, n0:n1].rearrange("p t (c i) -> p c t i", i=4),
+            )
+
+        def hand_on(g):
+            cols = slice(g * GROUP, (g + 1) * GROUP)
+            codes = keep.tile([P, GROUP], I32, name="out_codes%d" % g, align_bytes=64)
+            nc.vector.quantize_mx(out=codes[:].bitcast(FP8X4), scales=out_sc[:, cols], in_=res_bf[g][:])
+            nc.sync.dma_start(out=out_words[:, cols], in_=codes[:])
+
+        project(0)
+        project(1)
+        keep_h(0)
+        deal_weights(nc.vector.tensor_copy, w2_bf, w2_raw)
+        nc.vector.quantize_mx(out=w2_codes[:].bitcast(FP8X4), scales=w2_scales[:], in_=w2_bf[:])
+        quantise_g(0)
+        quantise_g(1)
+        keep_h(1)
+        branch(0)
+        project(2)
+        branch(1)
+        quantise_g(2)
+        keep_h(2)
+        project(3)
+        round_result(nc.vector.tensor_copy, 0, 0, GROUP)
+        branch(2)
+        quantise_g(3)
+        keep_h(3)
+        hand_on(0)
+        round_result(nc.vector.tensor_copy, 1, 0, GROUP)
+        branch(3)
+        round_result(nc.scalar.copy, 2, 0, GROUP)
+        hand_on(1)
+        round_result(nc.vector.tensor_copy, 3, 0, 160)
+        round_result(nc.scalar.copy, 3, 160, GROUP)
+        hand_on(2)
+        hand_on(3)
+        for q in range(4):
+            queue = nc.scalar if q < 2 else nc.sync
+            queue.dma_start(
+                out=out_2[0, 4 * q : 4 * q + 4, :].bitcast(I32),
+                in_=out_sc[32 * q : 32 * q + 4, :].bitcast(I32),
+            )

@@ -20,12 +20,13 @@ PASSES = K // (P * PACK)
 CHUNK = 128
 GROUP = 256
 HALF = 512
+W2_HEAD = 48
 FLOPS = 2 * K * H * S + 2 * H * H * S
 
 
-def deal_weights(engine_copy, grouped, raw):
+def deal_weights(engine_copy, grouped, raw, m0=0, m1=P):
     engine_copy(
-        out=grouped[:].rearrange("p (t m j) -> p m j t", t=PACK, j=PACK),
+        out=grouped[:].rearrange("p (t m j) -> p m j t", t=PACK, j=PACK)[:, m0:m1],
         in_=raw[:].rearrange("p j (m t) -> p m j t", t=PACK),
     )
 
@@ -41,8 +42,9 @@ def tile_picked_zres_silu_po_kernel(
 
         offsets = keep.tile([P, S // 16], U16, name="offsets")
         w1_raw = [keep.tile([P, PACK, H], F32, name="w1_raw%d" % o) for o in range(PASSES)]
-        w2_raw = keep.tile([P, PACK, H], F32, name="w2_raw")
-        word_table = [keep.tile([P, T], I32, name="word_table%d" % o) for o in range(PASSES)]
+        w2_head = keep.tile([P, PACK, W2_HEAD * PACK], F32, name="w2_head")
+        w2_rest = keep.tile([P, PACK, H - W2_HEAD * PACK], F32, name="w2_rest")
+        word_table = [keep.tile([P, T], I32, name="word_table%d" % o, tag="table%d" % o, align_bytes=64) for o in range(PASSES)]
         scale_table = keep.tile([P, T], U8, name="scale_table")
         turn_sb = keep.tile([P, PACK], F32, name="turn_sb")
 
@@ -56,34 +58,39 @@ def tile_picked_zres_silu_po_kernel(
         def load_words(o):
             nc.sync.dma_start(out=word_table[o][:], in_=x_words[o].rearrange("p n t -> p (n t)").bitcast(I32))
 
-        load_words(0)
+        def load_w1(o):
+            nc.sync.dma_start(out=w1_raw[o][:], in_=w1[512 * o : 512 * (o + 1), :].rearrange("(p j) c -> p j c", j=PACK))
+
+        load_w1(0)
         nc.sync.dma_start(offsets[:], offs)
         for q in range(4):
-            nc.sync.dma_start(
+            nc.gpsimd.dma_start(
                 out=scale_table[32 * q : 32 * q + 4 * PASSES, :].bitcast(I32),
                 in_=x_scales[:, 4 * q : 4 * q + 4, :].bitcast(I32),
             )
-        for o in range(PASSES):
-            nc.sync.dma_start(out=w1_raw[o][:], in_=w1[512 * o : 512 * (o + 1), :].rearrange("(p j) c -> p j c", j=PACK))
+        load_words(0)
+        load_w1(1)
         load_words(1)
-        nc.sync.dma_start(out=w2_raw[:], in_=w2.rearrange("(p j) c -> p j c", j=PACK))
+        w2_rows = w2.rearrange("(p j) c -> p j c", j=PACK)
+        nc.sync.dma_start(out=w2_head[:], in_=w2_rows[:, :, 0 : W2_HEAD * PACK])
+        nc.sync.dma_start(out=w2_rest[:], in_=w2_rows[:, :, W2_HEAD * PACK : H])
         nc.sync.dma_start(out=turn_sb[:], in_=turn.rearrange("(p t) o -> p (t o)", t=PACK))
 
+        w1_bf = [keep.tile([P, H * PACK], BF16, name="w1_bf%d" % o, tag="stage%d" % o, align_bytes=64) for o in range(PASSES)]
+        w1_codes = [keep.tile([P, H], U32, name="w1_codes%d" % o, align_bytes=64) for o in range(PASSES)]
+        w1_scales = [keep.tile([P, H], U8, name="w1_scales%d" % o, align_bytes=64) for o in range(PASSES)]
+
+        def quantise_w1(o):
+            nc.vector.quantize_mx(out=w1_codes[o][:].bitcast(FP8X4), scales=w1_scales[o][:], in_=w1_bf[o][:])
+
+        deal_weights(nc.scalar.copy, w1_bf[0], w1_raw[0])
+        quantise_w1(0)
         x_first = keep.tile([P, S], U32, name="x_first", align_bytes=64)
         nc.vector.tensor_copy(x_first[:], word_table[0][:].bitcast(U32).indirect(offsets[:]))
-        x_sc = keep.tile([P, S], U8, name="x_sc", align_bytes=64)
+        x_sc = keep.tile([P, S], U8, name="x_sc", tag="table0", align_bytes=64)
         nc.vector.tensor_copy(x_sc[:], scale_table[:].indirect(offsets[:]))
-
-        w1_bf = [keep.tile([P, H * PACK], BF16, name="w1_bf%d" % o, align_bytes=64) for o in range(PASSES)]
-        deal_weights(nc.scalar.copy, w1_bf[0], w1_raw[0])
-        deal_weights(nc.vector.tensor_copy, w1_bf[1], w1_raw[1])
-        w1_codes, w1_scales = [], []
-        for o in range(PASSES):
-            codes = keep.tile([P, H], U32, name="w1_codes%d" % o, align_bytes=64)
-            scales = keep.tile([P, H], U8, name="w1_scales%d" % o, align_bytes=64)
-            nc.vector.quantize_mx(out=codes[:].bitcast(FP8X4), scales=scales[:], in_=w1_bf[o][:])
-            w1_codes.append(codes)
-            w1_scales.append(scales)
+        deal_weights(nc.scalar.copy, w1_bf[1], w1_raw[1])
+        quantise_w1(1)
 
         x_second = []
         for hf in range(S // HALF):
@@ -93,13 +100,13 @@ def tile_picked_zres_silu_po_kernel(
             x_second.append(tile)
 
         warm_bank = yps.tile([P, 2, GROUP], F32, name="y_bank")
-        for rep in range(3):
+        for rep in range(4):
             nc.tensor.matmul_mx(
                 out=warm_bank[:].rearrange("p u n -> p (u n)"),
                 lhsT=w1_codes[1][:, 0:P].bitcast(FP8X4),
                 lhsT_scale=w1_scales[1][:, 0:P],
-                rhs=x_first[:, 0:HALF].bitcast(FP8X4),
-                rhs_scale=x_sc[:, 0:HALF],
+                rhs=w1_codes[1][:].bitcast(FP8X4),
+                rhs_scale=w1_scales[1][:],
                 start=True,
                 stop=True,
             )
@@ -149,7 +156,8 @@ def tile_picked_zres_silu_po_kernel(
 
         def keep_h(g):
             for c in range(GROUP // CHUNK):
-                nc.scalar.copy(out=h_sb[g][:, :, c * CHUNK : (c + 1) * CHUNK], in_=h_banks[(g, c)][:])
+                copy = nc.vector.tensor_copy if (g, c) == (1, 1) else nc.scalar.copy
+                copy(out=h_sb[g][:, :, c * CHUNK : (c + 1) * CHUNK], in_=h_banks[(g, c)][:])
 
         def quantise_g(g):
             nc.vector.quantize_mx(out=g_codes[g][:].bitcast(FP8X4), scales=g_scales[g][:], in_=g_bf[g][:])
@@ -175,7 +183,10 @@ def tile_picked_zres_silu_po_kernel(
                     nc.vector.scalar_tensor_tensor(
                         out=res[g][:, t, :], in0=bank[:, u, :], scalar=turn_sb[:, t : t + 1], in1=h_sb[g][:, t, :], op0=MULT, op1=ADD
                     )
-            nc.sync.dma_start(out=out_rows[:, :, cols], in_=res[g][:])
+                if g == groups - 1:
+                    nc.sync.dma_start(out=out_rows[:, 2 * pair : 2 * pair + 2, cols], in_=res[g][:, 2 * pair : 2 * pair + 2, :])
+            if g < groups - 1:
+                nc.sync.dma_start(out=out_rows[:, :, cols], in_=res[g][:])
 
         def round_result(copy, g, n0, n1):
             copy(
@@ -189,10 +200,11 @@ def tile_picked_zres_silu_po_kernel(
             nc.vector.quantize_mx(out=codes[:].bitcast(FP8X4), scales=out_sc[:, cols], in_=res_bf[g][:])
             nc.sync.dma_start(out=out_words[:, cols], in_=codes[:])
 
+        deal_weights(nc.scalar.copy, w2_bf, w2_head, 0, W2_HEAD)
         project(0)
         project(1)
         keep_h(0)
-        deal_weights(nc.vector.tensor_copy, w2_bf, w2_raw)
+        deal_weights(nc.vector.tensor_copy, w2_bf, w2_rest, W2_HEAD, P)
         nc.vector.quantize_mx(out=w2_codes[:].bitcast(FP8X4), scales=w2_scales[:], in_=w2_bf[:])
         quantise_g(0)
         quantise_g(1)
@@ -208,7 +220,7 @@ def tile_picked_zres_silu_po_kernel(
         quantise_g(3)
         keep_h(3)
         hand_on(0)
-        round_result(nc.vector.tensor_copy, 1, 0, GROUP)
+        round_result(nc.scalar.copy, 1, 0, GROUP)
         branch(3)
         round_result(nc.scalar.copy, 2, 0, GROUP)
         hand_on(1)

@@ -16,19 +16,37 @@ ADD = mybir.AluOpType.add
 P = 128
 PACK = 4
 K, T, S, H = 1024, 4096, 1024, 512
-PASSES = K // (P * PACK)
-CHUNK = 128
+PASS_ROWS = P * PACK
+PASSES = K // PASS_ROWS
+QUADRANT = 32
+BANK = 512
+BANKS = 8
+HALF = S // 2
+CHUNK = BANK // PACK
 GROUP = 256
-HALF = 512
+GROUPS = S // GROUP
+LINE = 4
+
+EARLY_SCALE_LOADS = 6
 W2_HEAD = 48
+LAST_VECTOR_TOKENS = 160
+
 FLOPS = 2 * K * H * S + 2 * H * H * S
 
 
-def deal_weights(engine_copy, grouped, raw, m0=0, m1=P):
-    engine_copy(
-        out=grouped[:].rearrange("p (t m j) -> p m j t", t=PACK, j=PACK)[:, m0:m1],
-        in_=raw[:].rearrange("p j (m t) -> p m j t", t=PACK),
+def deal_weights(copy, dealt, raw, m0, m1):
+    copy(
+        out=dealt[:].rearrange("p (t m j) -> p m t j", t=PACK, j=PACK)[:, m0:m1],
+        in_=raw[:].rearrange("p j (m t) -> p m t j", t=PACK),
     )
+
+
+def interleaved(flat):
+    return flat.rearrange("p (c i t) -> p c t i", i=LINE, t=PACK)
+
+
+def by_rows(rows):
+    return rows.rearrange("p t (c i) -> p c t i", i=LINE)
 
 
 def tile_picked_zres_silu_po_kernel(
@@ -37,200 +55,204 @@ def tile_picked_zres_silu_po_kernel(
     nc = tc.nc
     with ExitStack() as ctx:
         keep = ctx.enter_context(tc.tile_pool(name="keep", bufs=1))
-        hps = ctx.enter_context(tc.psum_pool(name="hps", bufs=4))
-        yps = ctx.enter_context(tc.psum_pool(name="yps", bufs=4))
+        psum = ctx.enter_context(tc.psum_pool(name="psum", bufs=BANKS))
+
+        def mx_tiles(name, width):
+            codes = keep.tile([P, width], U32, name=name + "_codes", align_bytes=64)
+            scales = keep.tile([P, width], U8, name=name + "_scales", align_bytes=64)
+            return codes, scales
+
+        def quantise(codes, scales, values):
+            nc.vector.quantize_mx(out=codes.bitcast(FP8X4), scales=scales, in_=values)
+
+        zero = keep.tile([P, 8], F32, name="zero")
+        silu_bias = keep.tile([P, 8], F32, name="silu_bias")
+        nc.vector.memset(zero[:], 0.0)
+        nc.scalar.activation(silu_bias[:], zero[:], SILU)
 
         offsets = keep.tile([P, S // 16], U16, name="offsets")
+        word_table = [keep.tile([P, T], I32, name="word_table%d" % o) for o in range(PASSES)]
         w1_raw = [keep.tile([P, PACK, H], F32, name="w1_raw%d" % o) for o in range(PASSES)]
         w2_head = keep.tile([P, PACK, W2_HEAD * PACK], F32, name="w2_head")
         w2_rest = keep.tile([P, PACK, H - W2_HEAD * PACK], F32, name="w2_rest")
-        word_table = [keep.tile([P, T], I32, name="word_table%d" % o, tag="table%d" % o, align_bytes=64) for o in range(PASSES)]
-        scale_table = keep.tile([P, T], U8, name="scale_table")
         turn_sb = keep.tile([P, PACK], F32, name="turn_sb")
 
-        warm = keep.tile([P, 8], F32, name="warm")
-        warm_out = keep.tile([P, 8], F32, name="warm_out")
-        nc.vector.memset(warm[:], 0.0)
-        nc.scalar.activation(warm_out[:], warm[:], SILU)
-
+        scale_table = keep.tile([P, T], U8, name="scale_table")
         nc.vector.memset(scale_table[:].bitcast(I32), 0)
 
         def load_words(o):
-            nc.sync.dma_start(out=word_table[o][:], in_=x_words[o].rearrange("p n t -> p (n t)").bitcast(I32))
+            nc.sync.dma_start(out=word_table[o][:], in_=x_words[o].rearrange("p n j -> p (n j)").bitcast(I32))
 
         def load_w1(o):
-            nc.sync.dma_start(out=w1_raw[o][:], in_=w1[512 * o : 512 * (o + 1), :].rearrange("(p j) c -> p j c", j=PACK))
+            rows = w1[PASS_ROWS * o : PASS_ROWS * (o + 1), :]
+            nc.sync.dma_start(out=w1_raw[o][:], in_=rows.rearrange("(p j) c -> p j c", j=PACK))
 
-        load_w1(0)
+        def load_scale_rows(first, last):
+            for index in range(first, last):
+                r, o = divmod(index, PASSES)
+                nc.sync.dma_start(
+                    out=scale_table[4 * o + r : P : QUADRANT, :].bitcast(I32),
+                    in_=x_scales[o].rearrange("(q r) n -> q r n", r=4)[:, r, :].bitcast(I32),
+                )
+
         nc.sync.dma_start(offsets[:], offs)
-        for q in range(4):
-            nc.gpsimd.dma_start(
-                out=scale_table[32 * q : 32 * q + 4 * PASSES, :].bitcast(I32),
-                in_=x_scales[:, 4 * q : 4 * q + 4, :].bitcast(I32),
-            )
         load_words(0)
+        load_scale_rows(0, EARLY_SCALE_LOADS)
+        load_w1(0)
+        load_scale_rows(EARLY_SCALE_LOADS, 4 * PASSES)
         load_w1(1)
         load_words(1)
         w2_rows = w2.rearrange("(p j) c -> p j c", j=PACK)
         nc.sync.dma_start(out=w2_head[:], in_=w2_rows[:, :, 0 : W2_HEAD * PACK])
         nc.sync.dma_start(out=w2_rest[:], in_=w2_rows[:, :, W2_HEAD * PACK : H])
-        nc.sync.dma_start(out=turn_sb[:], in_=turn.rearrange("(p t) o -> p (t o)", t=PACK))
+        nc.sync.dma_start(out=turn_sb[:], in_=turn.rearrange("(p t) one -> p (t one)", t=PACK))
 
-        w1_bf = [keep.tile([P, H * PACK], BF16, name="w1_bf%d" % o, tag="stage%d" % o, align_bytes=64) for o in range(PASSES)]
-        w1_codes = [keep.tile([P, H], U32, name="w1_codes%d" % o, align_bytes=64) for o in range(PASSES)]
-        w1_scales = [keep.tile([P, H], U8, name="w1_scales%d" % o, align_bytes=64) for o in range(PASSES)]
-
-        def quantise_w1(o):
-            nc.vector.quantize_mx(out=w1_codes[o][:].bitcast(FP8X4), scales=w1_scales[o][:], in_=w1_bf[o][:])
-
-        deal_weights(nc.scalar.copy, w1_bf[0], w1_raw[0])
-        quantise_w1(0)
+        w1_dealt = [keep.tile([P, H * PACK], BF16, name="w1_dealt%d" % o, align_bytes=64) for o in range(PASSES)]
+        w1_mx = [mx_tiles("w1_%d" % o, H) for o in range(PASSES)]
         x_first = keep.tile([P, S], U32, name="x_first", align_bytes=64)
+        x_picked_scales = keep.tile([P, S], U8, name="x_picked_scales", align_bytes=64)
+        x_last = [keep.tile([P, HALF], U32, name="x_last%d" % half, align_bytes=64) for half in range(2)]
+
         nc.vector.tensor_copy(x_first[:], word_table[0][:].bitcast(U32).indirect(offsets[:]))
-        x_sc = keep.tile([P, S], U8, name="x_sc", tag="table0", align_bytes=64)
-        nc.vector.tensor_copy(x_sc[:], scale_table[:].indirect(offsets[:]))
-        deal_weights(nc.scalar.copy, w1_bf[1], w1_raw[1])
-        quantise_w1(1)
+        deal_weights(nc.scalar.copy, w1_dealt[0], w1_raw[0], 0, P)
+        quantise(w1_mx[0][0][:], w1_mx[0][1][:], w1_dealt[0][:])
+        nc.vector.tensor_copy(x_picked_scales[:], scale_table[:].indirect(offsets[:]))
+        deal_weights(nc.scalar.copy, w1_dealt[1], w1_raw[1], 0, P)
+        quantise(w1_mx[1][0][:], w1_mx[1][1][:], w1_dealt[1][:])
+        for half in range(2):
+            entries = offsets[:, half * HALF // 16 : (half + 1) * HALF // 16]
+            nc.vector.tensor_copy(x_last[half][:], word_table[1][:].bitcast(U32).indirect(entries))
 
-        x_second = []
-        for hf in range(S // HALF):
-            tile = keep.tile([P, HALF], U32, name="x_second%d" % hf, align_bytes=64)
-            cols = slice(hf * HALF // 16, (hf + 1) * HALF // 16)
-            nc.vector.tensor_copy(tile[:], word_table[1][:].bitcast(U32).indirect(offsets[:, cols]))
-            x_second.append(tile)
-
-        warm_bank = yps.tile([P, 2, GROUP], F32, name="y_bank")
-        for rep in range(4):
+        def project_pass(out, t, o, n0, n1):
+            codes, scales = w1_mx[o]
+            words = x_first[:, n0:n1] if o == 0 else x_last[n0 // HALF][:, n0 % HALF : n0 % HALF + n1 - n0]
             nc.tensor.matmul_mx(
-                out=warm_bank[:].rearrange("p u n -> p (u n)"),
-                lhsT=w1_codes[1][:, 0:P].bitcast(FP8X4),
-                lhsT_scale=w1_scales[1][:, 0:P],
-                rhs=w1_codes[1][:].bitcast(FP8X4),
-                rhs_scale=w1_scales[1][:],
-                start=True,
-                stop=True,
+                out=out,
+                lhsT=codes[:, t * P : (t + 1) * P].bitcast(FP8X4),
+                lhsT_scale=scales[:, t * P : (t + 1) * P],
+                rhs=words.bitcast(FP8X4),
+                rhs_scale=x_picked_scales[4 * o : P, n0:n1],
+                start=(o == 0),
+                stop=(o == PASSES - 1),
             )
 
+        h_rows = [keep.tile([P, PACK, GROUP], F32, name="h_rows%d" % g) for g in range(GROUPS)]
+        g_values = [keep.tile([P, GROUP * PACK], BF16, name="g_values%d" % g, align_bytes=64) for g in range(GROUPS)]
+        g_mx = [mx_tiles("g%d" % g, GROUP) for g in range(GROUPS)]
+        result = [keep.tile([P, PACK, GROUP], F32, name="result%d" % g) for g in range(GROUPS)]
+        rounded = [keep.tile([P, GROUP * PACK], BF16, name="rounded%d" % g, align_bytes=64) for g in range(GROUPS)]
+        out_codes = [keep.tile([P, GROUP], I32, name="out_codes%d" % g, align_bytes=64) for g in range(GROUPS)]
+        out_scales = keep.tile([P, S], U8, name="out_scales", align_bytes=64)
+        w2_dealt = keep.tile([P, H * PACK], BF16, name="w2_dealt", align_bytes=64)
+        w2_codes, w2_scales = mx_tiles("w2", H)
         out_rows = out_0.rearrange("(p t) n -> p t n", t=PACK)
-        out_words = out_1[0].rearrange("p n t -> p (n t)").bitcast(I32)
-        out_sc = keep.tile([P, S], U8, name="out_sc", align_bytes=64)
+        out_words = out_1[0].rearrange("p n j -> p (n j)").bitcast(I32)
 
-        groups = S // GROUP
-        g_bf = [keep.tile([P, GROUP * PACK], BF16, name="g_bf%d" % g, align_bytes=64) for g in range(groups)]
-        g_codes = [keep.tile([P, GROUP], U32, name="g_codes%d" % g, align_bytes=64) for g in range(groups)]
-        g_scales = [keep.tile([P, GROUP], U8, name="g_scales%d" % g, align_bytes=64) for g in range(groups)]
-        h_sb = [keep.tile([P, PACK, GROUP], F32, name="h_sb%d" % g) for g in range(groups)]
-        res = [keep.tile([P, PACK, GROUP], F32, name="res%d" % g) for g in range(groups)]
-        res_bf = [keep.tile([P, GROUP * PACK], BF16, name="res_bf%d" % g, align_bytes=64) for g in range(groups)]
-        w2_bf = keep.tile([P, H * PACK], BF16, name="w2_bf", align_bytes=64)
-        w2_codes = keep.tile([P, H], U32, name="w2_codes", align_bytes=64)
-        w2_scales = keep.tile([P, H], U8, name="w2_scales", align_bytes=64)
-        h_banks = {}
+        wide_banks = [psum.tile([P, BANK], F32, name="bank") for t in range(PACK)]
+        for o in range(PASSES):
+            for t in range(PACK):
+                project_pass(wide_banks[t][:], t, o, 0, HALF)
 
-        def project(g):
+        def keep_h_wide(copy, g, t):
+            copy(out=h_rows[g][:, t, :], in_=wide_banks[t][:, g * GROUP : (g + 1) * GROUP])
+
+        def activate_wide(g):
+            nc.scalar.activation(interleaved(g_values[g][:]), by_rows(h_rows[g][:]), SILU, bias=silu_bias[:, 0:1])
+
+        chunk_banks = {}
+
+        def project_chunks(g):
             for c in range(GROUP // CHUNK):
                 n0 = g * GROUP + c * CHUNK
-                bank = hps.tile([P, PACK, CHUNK], F32, name="h_bank")
-                h_banks[(g, c)] = bank
+                bank = psum.tile([P, PACK, CHUNK], F32, name="bank")
+                chunk_banks[(g, c)] = bank
                 for t in range(PACK):
-                    m = slice(t * P, (t + 1) * P)
                     for o in range(PASSES):
-                        if o == 0:
-                            words = x_first[:, n0 : n0 + CHUNK]
-                        else:
-                            words = x_second[n0 // HALF][:, n0 % HALF : n0 % HALF + CHUNK]
-                        nc.tensor.matmul_mx(
-                            out=bank[:, t, :],
-                            lhsT=w1_codes[o][:, m].bitcast(FP8X4),
-                            lhsT_scale=w1_scales[o][:, m],
-                            rhs=words.bitcast(FP8X4),
-                            rhs_scale=x_sc[4 * o : P, n0 : n0 + CHUNK],
-                            start=(o == 0),
-                            stop=(o == PASSES - 1),
-                        )
+                        project_pass(bank[:, t, :], t, o, n0, n0 + CHUNK)
                 nc.scalar.activation(
-                    g_bf[g][:, c * CHUNK * PACK : (c + 1) * CHUNK * PACK].rearrange("p (n t) -> p n t", t=PACK),
+                    g_values[g][:, c * BANK : (c + 1) * BANK].rearrange("p (n t) -> p n t", t=PACK),
                     bank[:].rearrange("p t n -> p n t"),
                     SILU,
+                    bias=silu_bias[:, 0:1],
                 )
 
-        def keep_h(g):
+        def keep_h_chunks(g):
             for c in range(GROUP // CHUNK):
-                copy = nc.vector.tensor_copy if (g, c) == (1, 1) else nc.scalar.copy
-                copy(out=h_sb[g][:, :, c * CHUNK : (c + 1) * CHUNK], in_=h_banks[(g, c)][:])
+                nc.scalar.copy(out=h_rows[g][:, :, c * CHUNK : (c + 1) * CHUNK], in_=chunk_banks[(g, c)][:])
 
         def quantise_g(g):
-            nc.vector.quantize_mx(out=g_codes[g][:].bitcast(FP8X4), scales=g_scales[g][:], in_=g_bf[g][:])
+            quantise(g_mx[g][0][:], g_mx[g][1][:], g_values[g][:])
 
         def branch(g):
-            cols = slice(g * GROUP, (g + 1) * GROUP)
-            for pair in range(PACK // 2):
-                bank = yps.tile([P, 2, GROUP], F32, name="y_bank")
-                for u in range(2):
-                    t = 2 * pair + u
-                    m = slice(t * P, (t + 1) * P)
+            tokens = slice(g * GROUP, (g + 1) * GROUP)
+            for t0 in range(0, PACK, 2):
+                bank = psum.tile([P, 2, GROUP], F32, name="bank")
+                for t in (t0, t0 + 1):
                     nc.tensor.matmul_mx(
-                        out=bank[:, u, :],
-                        lhsT=w2_codes[:, m].bitcast(FP8X4),
-                        lhsT_scale=w2_scales[:, m],
-                        rhs=g_codes[g][:].bitcast(FP8X4),
-                        rhs_scale=g_scales[g][:],
+                        out=bank[:, t - t0, :],
+                        lhsT=w2_codes[:, t * P : (t + 1) * P].bitcast(FP8X4),
+                        lhsT_scale=w2_scales[:, t * P : (t + 1) * P],
+                        rhs=g_mx[g][0][:].bitcast(FP8X4),
+                        rhs_scale=g_mx[g][1][:],
                         start=True,
                         stop=True,
                     )
-                for u in range(2):
-                    t = 2 * pair + u
+                for t in (t0, t0 + 1):
                     nc.vector.scalar_tensor_tensor(
-                        out=res[g][:, t, :], in0=bank[:, u, :], scalar=turn_sb[:, t : t + 1], in1=h_sb[g][:, t, :], op0=MULT, op1=ADD
+                        out=result[g][:, t, :],
+                        in0=bank[:, t - t0, :],
+                        scalar=turn_sb[:, t : t + 1],
+                        in1=h_rows[g][:, t, :],
+                        op0=MULT,
+                        op1=ADD,
                     )
-                if g == groups - 1:
-                    nc.sync.dma_start(out=out_rows[:, 2 * pair : 2 * pair + 2, cols], in_=res[g][:, 2 * pair : 2 * pair + 2, :])
-            if g < groups - 1:
-                nc.sync.dma_start(out=out_rows[:, :, cols], in_=res[g][:])
+                if g == GROUPS - 1:
+                    nc.sync.dma_start(out=out_rows[:, t0 : t0 + 2, tokens], in_=result[g][:, t0 : t0 + 2, :])
+            if g < GROUPS - 1:
+                nc.sync.dma_start(out=out_rows[:, :, tokens], in_=result[g][:])
 
         def round_result(copy, g, n0, n1):
-            copy(
-                out=res_bf[g][:, n0 * PACK : n1 * PACK].rearrange("p (c i t) -> p c t i", i=4, t=PACK),
-                in_=res[g][:, :, n0:n1].rearrange("p t (c i) -> p c t i", i=4),
-            )
+            copy(out=interleaved(rounded[g][:, n0 * PACK : n1 * PACK]), in_=by_rows(result[g][:, :, n0:n1]))
 
         def hand_on(g):
-            cols = slice(g * GROUP, (g + 1) * GROUP)
-            codes = keep.tile([P, GROUP], I32, name="out_codes%d" % g, align_bytes=64)
-            nc.vector.quantize_mx(out=codes[:].bitcast(FP8X4), scales=out_sc[:, cols], in_=res_bf[g][:])
-            nc.sync.dma_start(out=out_words[:, cols], in_=codes[:])
+            tokens = slice(g * GROUP, (g + 1) * GROUP)
+            quantise(out_codes[g][:], out_scales[:, tokens], rounded[g][:])
+            nc.sync.dma_start(out=out_words[:, tokens], in_=out_codes[g][:])
 
-        deal_weights(nc.scalar.copy, w2_bf, w2_head, 0, W2_HEAD)
-        project(0)
-        project(1)
-        keep_h(0)
-        deal_weights(nc.vector.tensor_copy, w2_bf, w2_rest, W2_HEAD, P)
-        nc.vector.quantize_mx(out=w2_codes[:].bitcast(FP8X4), scales=w2_scales[:], in_=w2_bf[:])
+        deal_weights(nc.scalar.copy, w2_dealt, w2_head, 0, W2_HEAD)
+        for t in range(PACK):
+            keep_h_wide(nc.vector.tensor_copy if t < 2 else nc.scalar.copy, 0, t)
+        activate_wide(0)
+        for t in range(PACK):
+            keep_h_wide(nc.scalar.copy, 1, t)
+        activate_wide(1)
+        deal_weights(nc.vector.tensor_copy, w2_dealt, w2_rest, W2_HEAD, P)
+        quantise(w2_codes[:], w2_scales[:], w2_dealt[:])
         quantise_g(0)
-        quantise_g(1)
-        keep_h(1)
+        project_chunks(2)
         branch(0)
-        project(2)
-        branch(1)
-        quantise_g(2)
-        keep_h(2)
-        project(3)
+        quantise_g(1)
+        keep_h_chunks(2)
+        project_chunks(3)
         round_result(nc.vector.tensor_copy, 0, 0, GROUP)
-        branch(2)
+        quantise_g(2)
+        branch(1)
         quantise_g(3)
-        keep_h(3)
+        keep_h_chunks(3)
+        branch(2)
         hand_on(0)
         round_result(nc.scalar.copy, 1, 0, GROUP)
         branch(3)
         round_result(nc.scalar.copy, 2, 0, GROUP)
         hand_on(1)
-        round_result(nc.vector.tensor_copy, 3, 0, 160)
-        round_result(nc.scalar.copy, 3, 160, GROUP)
+        round_result(nc.vector.tensor_copy, 3, 0, LAST_VECTOR_TOKENS)
+        round_result(nc.scalar.copy, 3, LAST_VECTOR_TOKENS, GROUP)
         hand_on(2)
         hand_on(3)
-        for q in range(4):
+
+        for q in range(P // QUADRANT):
             queue = nc.scalar if q < 2 else nc.sync
             queue.dma_start(
                 out=out_2[0, 4 * q : 4 * q + 4, :].bitcast(I32),
-                in_=out_sc[32 * q : 32 * q + 4, :].bitcast(I32),
+                in_=out_scales[QUADRANT * q : QUADRANT * q + 4, :].bitcast(I32),
             )

from contextlib import ExitStack

import concourse.mybir as mybir

F32 = mybir.dt.float32
BF16 = mybir.dt.bfloat16
I32 = mybir.dt.int32
U32 = mybir.dt.uint32
U16 = mybir.dt.uint16
U8 = mybir.dt.uint8
FP8X4 = mybir.dt.float8_e4m3fn_x4
SILU = mybir.ActivationFunctionType.Silu
MULT = mybir.AluOpType.mult
ADD = mybir.AluOpType.add

P = 128
PACK = 4
K, T, S, H = 1024, 4096, 1024, 512
PASS_ROWS = P * PACK
PASSES = K // PASS_ROWS
QUADRANT = 32
BANK = 512
BANKS = 8
HALF = S // 2
CHUNK = BANK // PACK
GROUP = 256
GROUPS = S // GROUP
LINE = 4

EARLY_SCALE_LOADS = 6
W2_HEAD = 48
LAST_VECTOR_TOKENS = 160

FLOPS = 2 * K * H * S + 2 * H * H * S


def deal_weights(copy, dealt, raw, m0, m1):
    copy(
        out=dealt[:].rearrange("p (t m j) -> p m t j", t=PACK, j=PACK)[:, m0:m1],
        in_=raw[:].rearrange("p j (m t) -> p m t j", t=PACK),
    )


def interleaved(flat):
    return flat.rearrange("p (c i t) -> p c t i", i=LINE, t=PACK)


def by_rows(rows):
    return rows.rearrange("p t (c i) -> p c t i", i=LINE)


def tile_picked_zres_silu_po_kernel(
    tc, x_words, x_scales, w1, w2, turn, offs, out_0, out_1, out_2
):
    nc = tc.nc
    with ExitStack() as ctx:
        keep = ctx.enter_context(tc.tile_pool(name="keep", bufs=1))
        psum = ctx.enter_context(tc.psum_pool(name="psum", bufs=BANKS))

        def mx_tiles(name, width):
            codes = keep.tile([P, width], U32, name=name + "_codes", align_bytes=64)
            scales = keep.tile([P, width], U8, name=name + "_scales", align_bytes=64)
            return codes, scales

        def quantise(codes, scales, values):
            nc.vector.quantize_mx(out=codes.bitcast(FP8X4), scales=scales, in_=values)

        zero = keep.tile([P, 8], F32, name="zero")
        silu_bias = keep.tile([P, 8], F32, name="silu_bias")
        nc.vector.memset(zero[:], 0.0)
        nc.scalar.activation(silu_bias[:], zero[:], SILU)

        offsets = keep.tile([P, S // 16], U16, name="offsets")
        word_table = [keep.tile([P, T], I32, name="word_table%d" % o) for o in range(PASSES)]
        w1_raw = [keep.tile([P, PACK, H], F32, name="w1_raw%d" % o) for o in range(PASSES)]
        w2_head = keep.tile([P, PACK, W2_HEAD * PACK], F32, name="w2_head")
        w2_rest = keep.tile([P, PACK, H - W2_HEAD * PACK], F32, name="w2_rest")
        turn_sb = keep.tile([P, PACK], F32, name="turn_sb")

        scale_table = keep.tile([P, T], U8, name="scale_table")
        nc.vector.memset(scale_table[:].bitcast(I32), 0)

        def load_words(o):
            nc.sync.dma_start(out=word_table[o][:], in_=x_words[o].rearrange("p n j -> p (n j)").bitcast(I32))

        def load_w1(o):
            rows = w1[PASS_ROWS * o : PASS_ROWS * (o + 1), :]
            nc.sync.dma_start(out=w1_raw[o][:], in_=rows.rearrange("(p j) c -> p j c", j=PACK))

        def load_scale_rows(first, last):
            for index in range(first, last):
                r, o = divmod(index, PASSES)
                nc.sync.dma_start(
                    out=scale_table[4 * o + r : P : QUADRANT, :].bitcast(I32),
                    in_=x_scales[o].rearrange("(q r) n -> q r n", r=4)[:, r, :].bitcast(I32),
                )

        nc.sync.dma_start(offsets[:], offs)
        load_words(0)
        load_scale_rows(0, EARLY_SCALE_LOADS)
        load_w1(0)
        load_scale_rows(EARLY_SCALE_LOADS, 4 * PASSES)
        load_w1(1)
        load_words(1)
        w2_rows = w2.rearrange("(p j) c -> p j c", j=PACK)
        nc.sync.dma_start(out=w2_head[:], in_=w2_rows[:, :, 0 : W2_HEAD * PACK])
        nc.sync.dma_start(out=w2_rest[:], in_=w2_rows[:, :, W2_HEAD * PACK : H])
        nc.sync.dma_start(out=turn_sb[:], in_=turn.rearrange("(p t) one -> p (t one)", t=PACK))

        w1_dealt = [keep.tile([P, H * PACK], BF16, name="w1_dealt%d" % o, align_bytes=64) for o in range(PASSES)]
        w1_mx = [mx_tiles("w1_%d" % o, H) for o in range(PASSES)]
        x_first = keep.tile([P, S], U32, name="x_first", align_bytes=64)
        x_picked_scales = keep.tile([P, S], U8, name="x_picked_scales", align_bytes=64)
        x_last = [keep.tile([P, HALF], U32, name="x_last%d" % half, align_bytes=64) for half in range(2)]

        nc.vector.tensor_copy(x_first[:], word_table[0][:].bitcast(U32).indirect(offsets[:]))
        deal_weights(nc.scalar.copy, w1_dealt[0], w1_raw[0], 0, P)
        quantise(w1_mx[0][0][:], w1_mx[0][1][:], w1_dealt[0][:])
        nc.vector.tensor_copy(x_picked_scales[:], scale_table[:].indirect(offsets[:]))
        deal_weights(nc.scalar.copy, w1_dealt[1], w1_raw[1], 0, P)
        quantise(w1_mx[1][0][:], w1_mx[1][1][:], w1_dealt[1][:])
        for half in range(2):
            entries = offsets[:, half * HALF // 16 : (half + 1) * HALF // 16]
            nc.vector.tensor_copy(x_last[half][:], word_table[1][:].bitcast(U32).indirect(entries))

        def project_pass(out, t, o, n0, n1):
            codes, scales = w1_mx[o]
            words = x_first[:, n0:n1] if o == 0 else x_last[n0 // HALF][:, n0 % HALF : n0 % HALF + n1 - n0]
            nc.tensor.matmul_mx(
                out=out,
                lhsT=codes[:, t * P : (t + 1) * P].bitcast(FP8X4),
                lhsT_scale=scales[:, t * P : (t + 1) * P],
                rhs=words.bitcast(FP8X4),
                rhs_scale=x_picked_scales[4 * o : P, n0:n1],
                start=(o == 0),
                stop=(o == PASSES - 1),
            )

        h_rows = [keep.tile([P, PACK, GROUP], F32, name="h_rows%d" % g) for g in range(GROUPS)]
        g_values = [keep.tile([P, GROUP * PACK], BF16, name="g_values%d" % g, align_bytes=64) for g in range(GROUPS)]
        g_mx = [mx_tiles("g%d" % g, GROUP) for g in range(GROUPS)]
        result = [keep.tile([P, PACK, GROUP], F32, name="result%d" % g) for g in range(GROUPS)]
        rounded = [keep.tile([P, GROUP * PACK], BF16, name="rounded%d" % g, align_bytes=64) for g in range(GROUPS)]
        out_codes = [keep.tile([P, GROUP], I32, name="out_codes%d" % g, align_bytes=64) for g in range(GROUPS)]
        out_scales = keep.tile([P, S], U8, name="out_scales", align_bytes=64)
        w2_dealt = keep.tile([P, H * PACK], BF16, name="w2_dealt", align_bytes=64)
        w2_codes, w2_scales = mx_tiles("w2", H)
        out_rows = out_0.rearrange("(p t) n -> p t n", t=PACK)
        out_words = out_1[0].rearrange("p n j -> p (n j)").bitcast(I32)

        wide_banks = [psum.tile([P, BANK], F32, name="bank") for t in range(PACK)]
        for o in range(PASSES):
            for t in range(PACK):
                project_pass(wide_banks[t][:], t, o, 0, HALF)

        def keep_h_wide(copy, g, t):
            copy(out=h_rows[g][:, t, :], in_=wide_banks[t][:, g * GROUP : (g + 1) * GROUP])

        def activate_wide(g):
            nc.scalar.activation(interleaved(g_values[g][:]), by_rows(h_rows[g][:]), SILU, bias=silu_bias[:, 0:1])

        chunk_banks = {}

        def project_chunks(g):
            for c in range(GROUP // CHUNK):
                n0 = g * GROUP + c * CHUNK
                bank = psum.tile([P, PACK, CHUNK], F32, name="bank")
                chunk_banks[(g, c)] = bank
                for t in range(PACK):
                    for o in range(PASSES):
                        project_pass(bank[:, t, :], t, o, n0, n0 + CHUNK)
                nc.scalar.activation(
                    g_values[g][:, c * BANK : (c + 1) * BANK].rearrange("p (n t) -> p n t", t=PACK),
                    bank[:].rearrange("p t n -> p n t"),
                    SILU,
                    bias=silu_bias[:, 0:1],
                )

        def keep_h_chunks(g):
            for c in range(GROUP // CHUNK):
                nc.scalar.copy(out=h_rows[g][:, :, c * CHUNK : (c + 1) * CHUNK], in_=chunk_banks[(g, c)][:])

        def quantise_g(g):
            quantise(g_mx[g][0][:], g_mx[g][1][:], g_values[g][:])

        def branch(g):
            tokens = slice(g * GROUP, (g + 1) * GROUP)
            for t0 in range(0, PACK, 2):
                bank = psum.tile([P, 2, GROUP], F32, name="bank")
                for t in (t0, t0 + 1):
                    nc.tensor.matmul_mx(
                        out=bank[:, t - t0, :],
                        lhsT=w2_codes[:, t * P : (t + 1) * P].bitcast(FP8X4),
                        lhsT_scale=w2_scales[:, t * P : (t + 1) * P],
                        rhs=g_mx[g][0][:].bitcast(FP8X4),
                        rhs_scale=g_mx[g][1][:],
                        start=True,
                        stop=True,
                    )
                for t in (t0, t0 + 1):
                    nc.vector.scalar_tensor_tensor(
                        out=result[g][:, t, :],
                        in0=bank[:, t - t0, :],
                        scalar=turn_sb[:, t : t + 1],
                        in1=h_rows[g][:, t, :],
                        op0=MULT,
                        op1=ADD,
                    )
                if g == GROUPS - 1:
                    nc.sync.dma_start(out=out_rows[:, t0 : t0 + 2, tokens], in_=result[g][:, t0 : t0 + 2, :])
            if g < GROUPS - 1:
                nc.sync.dma_start(out=out_rows[:, :, tokens], in_=result[g][:])

        def round_result(copy, g, n0, n1):
            copy(out=interleaved(rounded[g][:, n0 * PACK : n1 * PACK]), in_=by_rows(result[g][:, :, n0:n1]))

        def hand_on(g):
            tokens = slice(g * GROUP, (g + 1) * GROUP)
            quantise(out_codes[g][:], out_scales[:, tokens], rounded[g][:])
            nc.sync.dma_start(out=out_words[:, tokens], in_=out_codes[g][:])

        deal_weights(nc.scalar.copy, w2_dealt, w2_head, 0, W2_HEAD)
        for t in range(PACK):
            keep_h_wide(nc.vector.tensor_copy if t < 2 else nc.scalar.copy, 0, t)
        activate_wide(0)
        for t in range(PACK):
            keep_h_wide(nc.scalar.copy, 1, t)
        activate_wide(1)
        deal_weights(nc.vector.tensor_copy, w2_dealt, w2_rest, W2_HEAD, P)
        quantise(w2_codes[:], w2_scales[:], w2_dealt[:])
        quantise_g(0)
        project_chunks(2)
        branch(0)
        quantise_g(1)
        keep_h_chunks(2)
        project_chunks(3)
        round_result(nc.vector.tensor_copy, 0, 0, GROUP)
        quantise_g(2)
        branch(1)
        quantise_g(3)
        keep_h_chunks(3)
        branch(2)
        hand_on(0)
        round_result(nc.scalar.copy, 1, 0, GROUP)
        branch(3)
        round_result(nc.scalar.copy, 2, 0, GROUP)
        hand_on(1)
        round_result(nc.vector.tensor_copy, 3, 0, LAST_VECTOR_TOKENS)
        round_result(nc.scalar.copy, 3, LAST_VECTOR_TOKENS, GROUP)
        hand_on(2)
        hand_on(3)

        for q in range(P // QUADRANT):
            queue = nc.scalar if q < 2 else nc.sync
            queue.dma_start(
                out=out_2[0, 4 * q : 4 * q + 4, :].bitcast(I32),
                in_=out_scales[QUADRANT * q : QUADRANT * q + 4, :].bitcast(I32),
            )
